import numpy as np
import ml_dtypes


def mxq(x, axis, fmt="e4m3"):
    dtype, down = {"e4m3": (ml_dtypes.float8_e4m3fn, 7), "e5m2": (ml_dtypes.float8_e5m2, 14)}[fmt]
    v = np.moveaxis(np.asarray(x, np.float32).astype(ml_dtypes.bfloat16).astype(np.float64), axis, -1)
    blocks = v.reshape(v.shape[:-1] + (-1, 32))
    amax = np.abs(blocks).max(-1, keepdims=True)
    byte = np.maximum(np.where(amax > 0, np.frexp(amax)[1] - 1 + 127, 0) - down, 1)
    scale = np.exp2(byte - 127.0)
    codes = (blocks / scale).astype(np.float32).astype(dtype).astype(np.float64)
    return np.moveaxis((codes * scale).reshape(v.shape), -1, axis)


WIDE = False


def mx_kscale(k):
    if not WIDE:
        return np.ones(k)
    levels = np.array([10, -10, 5, -5, 0])
    if k % 512:
        return np.exp2(np.random.permutation(np.resize(levels, k // 32))).repeat(32)
    a = np.empty((k // 512, 16))
    for p in range(k // 512):
        a[p, :8] = np.random.permutation(np.resize(levels, 8))
        for g in range(8):
            far = levels[np.abs(levels - a[p, g]) >= 10]
            a[p, g + 8] = far[np.random.randint(len(far))]
    return np.exp2(a.ravel()).repeat(32)


def f64(x):
    return np.asarray(x).astype(np.float64)


def striped(idx):
    return np.tile(idx.reshape(-1, 16).T, (8, 1)).astype(np.uint16)


def unstriped(offs):
    return offs[:16].T.reshape(-1).astype(np.int64)


def pack_weight(w):
    k, n = w.shape
    w = f64(np.asarray(w, np.float32).astype(ml_dtypes.bfloat16)).reshape(k // 32, 32, n)
    amax = np.abs(w).max(1)
    byte = np.clip(np.where(amax > 0, np.frexp(amax)[1] - 1 + 127 - 7, 1), 1, 254)
    scaled = (w * np.exp2(127.0 - byte)[:, None, :]).reshape(k, n).astype(np.float32)
    words = np.ascontiguousarray(scaled.reshape(k // 512, 128, 4, n).transpose(0, 1, 3, 2)).astype(ml_dtypes.float8_e4m3fn).view(np.uint8)
    return words, np.ascontiguousarray(byte.astype(np.uint8).reshape(k // 512, 16, n))


def unpack_weight(words, scales):
    g, p, n, _ = words.shape
    vals = np.ascontiguousarray(words).view(ml_dtypes.float8_e4m3fn).astype(np.float64) * np.repeat(np.exp2(scales.astype(np.float64) - 127.0), 8, axis=1)[..., None]
    return vals.transpose(0, 1, 3, 2).reshape(g * 512, n)


def sigmoid(v):
    return 1.0 / (1.0 + np.exp(-np.maximum(v, -700.0)))


K, T, S, D, N, H, V, U = 1024, 2048, 512, 2, 128, 512, 256, 512


def setup_inputs():
    n = np.random.standard_normal
    s = mx_kscale(K)[:, None]
    u = mx_kscale(H)
    packed_xT = pack_weight(n((K, T)) * s)
    return {
        "x_words": packed_xT[0],
        "x_scales": packed_xT[1],
        "hT": (n((K, H)) / np.sqrt(K) / s).astype(np.float32),
        "own": (0.7 * n((H, U))).astype(np.float32),
        "unit": (np.random.uniform(0.6, 1.4, (H, 1)) * u[:, None]).astype(np.float32),
        "w1": (n((H, N)) / np.sqrt(H) / u[:, None]).astype(np.float32),
        "offs": striped(np.random.permutation(T)[:S]),
        "ven": striped(np.random.permutation(np.concatenate([np.arange(V), np.random.randint(0, V, U - V)]))),
        "coc": striped(np.random.permutation(U)),
    }


def reference(x_words, x_scales, hT, own, unit, w1, offs, ven, coc):
    hTq = mxq(f64(hT), 0, "e4m3")
    xq = unpack_weight(x_words, x_scales)[:, unstriped(offs)]
    y = hTq.T @ xq
    aff = np.tanh(y)
    venue = aff.reshape(len(aff), -1, D).max(axis=2)
    vv = venue[:, unstriped(ven)]
    hv = vv + f64(own)
    hid = f64(unit) * (hv * (sigmoid(hv[:, unstriped(coc)])))
    return mxq(f64(w1), 0, "e4m3").T @ mxq(hid, 0, "e4m3")

@@ -1,0 +1,223 @@
+from contextlib import ExitStack
+
+import concourse.mybir as mybir
+
+K, T, S, N, H, V = 1024, 2048, 512, 128, 512, 256
+
+F32 = mybir.dt.float32
+BF16 = mybir.dt.bfloat16
+I32 = mybir.dt.int32
+U32 = mybir.dt.uint32
+U16 = mybir.dt.uint16
+U8 = mybir.dt.uint8
+FP8X4 = mybir.dt.float8_e4m3fn_x4
+ALU = mybir.AluOpType
+ACT = mybir.ActivationFunctionType
+
+P = 128
+PACK = 4
+PASSES = K // (P * PACK)
+PIECES = 2
+PIECE = S // PIECES
+
+FLOPS = 2 * K * H * S + 2 * H * N * S
+
+
+def tile_picked_yhlgnn_gate_p_kernel(
+    tc, x_words, x_scales, hT, own, unit, w1, offs, ven, coc, out
+):
+    nc = tc.nc
+    with ExitStack() as ctx:
+        held = ctx.enter_context(tc.tile_pool(name="held", bufs=1))
+        psum = ctx.enter_context(tc.psum_pool(name="psum", bufs=1))
+
+        offs_sb = held.tile([P, S // 16], U16, name="offs_sb")
+        ven_sb = held.tile([P, S // 16], U16, name="ven_sb")
+        coc_sb = held.tile([P, S // 16], U16, name="coc_sb")
+        h_raw = [held.tile([P, PACK, H], F32, name=f"h_raw{o}") for o in range(PASSES)]
+        words = [held.tile([P, T], U32, name=f"words{o}") for o in range(PASSES)]
+        scales = held.tile([P, T], U8, name="scales")
+        hv_own = [held.tile([P, 2 * S], F32, name=f"hv_own{t}") for t in range(PACK)]
+        w_raw = held.tile([P, PACK, N], F32, name="w_raw")
+        unit_sb = held.tile([P, PACK], F32, name="unit_sb")
+
+        own_rows = own.rearrange("(p t) j -> p t j", t=PACK)
+
+        def load_h(o):
+            rows = hT[o * P * PACK : (o + 1) * P * PACK, :]
+            nc.sync.dma_start(out=h_raw[o][:], in_=rows.rearrange("(p j) c -> p j c", j=PACK))
+
+        def load_words(o):
+            src = x_words[o].rearrange("p c r -> p (c r)").bitcast(I32)
+            nc.sync.dma_start(out=words[o][:].bitcast(I32), in_=src)
+
+        def load_own(t):
+            nc.sync.dma_start(out=hv_own[t][:, S:], in_=own_rows[:, t, :])
+
+        nc.gpsimd.memset(scales[:].bitcast(I32), 0)
+        load_h(0)
+        for q in range(4):
+            nc.gpsimd.dma_start(
+                out=scales[32 * q : 32 * q + 4 * PASSES, :].bitcast(I32),
+                in_=x_scales[:, 4 * q : 4 * q + 4, :].bitcast(I32),
+            )
+        nc.sync.dma_start(offs_sb[:], offs)
+        load_words(0)
+        load_h(1)
+        load_words(1)
+        nc.sync.dma_start(out=w_raw[:], in_=w1.rearrange("(p j) n -> p j n", j=PACK))
+        nc.sync.dma_start(ven_sb[:], ven)
+        load_own(0)
+        nc.sync.dma_start(coc_sb[:], coc)
+        load_own(1)
+        nc.sync.dma_start(out=unit_sb[:], in_=unit.rearrange("(p t) o -> p (t o)", t=PACK))
+        for t in range(2, PACK):
+            load_own(t)
+
+        h_bf = [held.tile([P, PACK * H], BF16, name=f"h_bf{o}", align_bytes=64) for o in range(PASSES)]
+        h_codes = [held.tile([P, H], U32, name=f"h_codes{o}", align_bytes=64) for o in range(PASSES)]
+        h_scales = [held.tile([P, H], U8, name=f"h_scales{o}", align_bytes=64) for o in range(PASSES)]
+        x_codes = [held.tile([P, S], U32, name=f"x_codes{o}", align_bytes=64) for o in range(PASSES)]
+        x_bytes = held.tile([P, S], U8, name="x_bytes", align_bytes=64)
+
+        def deal_h(o):
+            dst = h_bf[o][:].rearrange("p (t m j) -> p m j t", t=PACK, j=PACK)
+            src = h_raw[o][:].rearrange("p j (m t) -> p m j t", t=PACK)
+            nc.vector.tensor_copy(dst[:, :, :, : PACK - 1], src[:, :, :, : PACK - 1])
+            nc.scalar.copy(dst[:, :, :, PACK - 1], src[:, :, :, PACK - 1])
+
+        def quantize(codes, scale_bytes, values):
+            nc.vector.quantize_mx(out=codes.bitcast(FP8X4), scales=scale_bytes, in_=values)
+
+        halves = [slice(0, S // 2), slice(S // 2, S)]
+        spans = [(0, halves[0]), (1, halves[0]), (0, halves[1]), (1, halves[1]), (2, slice(0, S)), (3, slice(0, S))]
+        y = [psum.tile([P, c.stop - c.start], F32, name=f"y{k}") for k, (t, c) in enumerate(spans)]
+
+        def scores(o):
+            for k, (t, c) in enumerate(spans):
+                cols = slice(t * P, (t + 1) * P)
+                nc.tensor.matmul_mx(
+                    out=y[k][:],
+                    lhsT=h_codes[o][:, cols].bitcast(FP8X4),
+                    lhsT_scale=h_scales[o][:, cols],
+                    rhs=x_codes[o][:, c].bitcast(FP8X4),
+                    rhs_scale=x_bytes[4 * o :, c],
+                    start=(o == 0),
+                    stop=(o == PASSES - 1),
+                )
+
+        deal_h(0)
+        quantize(h_codes[0][:], h_scales[0][:], h_bf[0][:])
+        nc.vector.tensor_copy(x_codes[0][:], words[0][:].indirect(offs_sb[:]))
+        nc.vector.tensor_copy(x_bytes[:], scales[:].indirect(offs_sb[:]))
+        scores(0)
+        deal_h(1)
+        quantize(h_codes[1][:], h_scales[1][:], h_bf[1][:])
+        for c in halves:
+            nc.vector.tensor_copy(x_codes[1][:, c], words[1][:].indirect(offs_sb[:, c.start // 16 : c.stop // 16]))
+        scores(1)
+
+        venue_aff = [held.tile([P, V + S], F32, name=f"venue_aff{t}") for t in range(PACK)]
+        gate = [held.tile([P, S], F32, name=f"gate{t}") for t in range(PACK)]
+        picked = held.tile([P, S], F32, name="picked")
+        hid_rows = held.tile([P, PACK, S], BF16, name="hid_rows")
+        widths = [256,128,128]
+        starts = [sum(widths[:a]) for a in range(len(widths))]
+        whole = slice(0, S)
+        piece = [slice(c, c + w) for c, w in zip(starts, widths)]
+
+        def bound(k):
+            t, c = spans[k]
+            nc.scalar.activation(venue_aff[t][:, V + c.start : V + c.stop], y[k][:], ACT.Tanh)
+
+        def larger(t):
+            pairs = venue_aff[t][:, V:].rearrange("p (v d) -> p d v", d=2)
+            nc.vector.tensor_tensor(venue_aff[t][:, :V], pairs[:, 0, :], pairs[:, 1, :], ALU.max)
+
+        def fetch_add(t):
+            nc.vector.tensor_tensor(
+                hv_own[t][:, :S], venue_aff[t][:].indirect(ven_sb[:]), hv_own[t][:, S:], ALU.add
+            )
+
+        def fetch(t):
+            nc.scalar.activation(picked[:], venue_aff[t][:].indirect(ven_sb[:]), ACT.Copy)
+
+        def add(t):
+            nc.vector.tensor_tensor(hv_own[t][:, :S], picked[:], hv_own[t][:, S:], ALU.add)
+
+        def gates(t, cols):
+            entries = coc_sb[:, cols.start // 16 : cols.stop // 16]
+            nc.scalar.activation(gate[t][:, cols], hv_own[t][:].indirect(entries), ACT.Sigmoid)
+
+        def hidden(t, cols):
+            nc.vector.scalar_tensor_tensor(
+                out=hid_rows[:, t, cols],
+                in0=hv_own[t][:, cols],
+                scalar=unit_sb[:, t : t + 1],
+                in1=gate[t][:, cols],
+                op0=ALU.mult,
+                op1=ALU.mult,
+            )
+
+        def interleave(copy, dst, src):
+            copy(
+                dst.rearrange("p (c i t) -> p c t i", i=4, t=PACK),
+                src.rearrange("p t (c i) -> p c t i", i=4),
+            )
+
+        w_bf = held.tile([P, PACK * N], BF16, name="w_bf", align_bytes=64)
+        w_codes = held.tile([P, N], U32, name="w_codes", align_bytes=64)
+        w_scales = held.tile([P, N], U8, name="w_scales", align_bytes=64)
+        hid_bf = [held.tile([P, PACK * w], BF16, name=f"hid_bf{a}", align_bytes=64) for a, w in enumerate(widths)]
+        hid_codes = [held.tile([P, w], U32, name=f"hid_codes{a}", align_bytes=64) for a, w in enumerate(widths)]
+        hid_scales = [held.tile([P, w], U8, name=f"hid_scales{a}", align_bytes=64) for a, w in enumerate(widths)]
+
+        def weave(a, copy):
+            interleave(copy, hid_bf[a][:], hid_rows[:, :, piece[a]])
+
+        def finish(a):
+            quantize(hid_codes[a][:], hid_scales[a][:], hid_bf[a][:])
+            acc = psum.tile([P, widths[a]], F32, name=f"acc{a}", tag=f"y{a}")
+            nc.tensor.matmul_mx(
+                out=acc[:],
+                lhsT=w_codes[:].bitcast(FP8X4),
+                lhsT_scale=w_scales[:],
+                rhs=hid_codes[a][:].bitcast(FP8X4),
+                rhs_scale=hid_scales[a][:],
+                start=True,
+                stop=True,
+            )
+            result = held.tile([P, widths[a]], F32, name=f"result{a}")
+            nc.scalar.copy(result[:], acc[:])
+            nc.sync.dma_start(out=out[:, piece[a]], in_=result[:])
+
+        interleave(nc.vector.tensor_copy, w_bf[:], w_raw[:])
+        for k in range(len(spans)): bound(k)
+        quantize(w_codes[:], w_scales[:], w_bf[:])
+        larger(0)
+        larger(1)
+        fetch_add(0)
+        larger(2)
+        fetch_add(1)
+        gates(0, whole)
+        fetch(2)
+        larger(3)
+        fetch_add(3)
+        gates(1, whole)
+        add(2)
+        hidden(0, whole)
+        gates(3, piece[0])
+        gates(2, piece[0])
+        hidden(1, whole)
+        gates(3, halves[1])
+        hidden(3, piece[0])
+        hidden(2, piece[0])
+        gates(2, halves[1])
+        weave(0, nc.vector.tensor_copy)
+        hidden(3, halves[1])
+        hidden(2, halves[1])
+        weave(1, nc.scalar.copy)
+        finish(0)
+        weave(2, nc.vector.tensor_copy)
+        finish(1)
+        finish(2)

@@ -57,7 +57,7 @@ def tile_picked_yhlgnn_gate_p_kernel(
         nc.gpsimd.memset(scales[:].bitcast(I32), 0)
         load_h(0)
         for q in range(4):
-            nc.gpsimd.dma_start(
+            nc.sync.dma_start(
                 out=scales[32 * q : 32 * q + 4 * PASSES, :].bitcast(I32),
                 in_=x_scales[:, 4 * q : 4 * q + 4, :].bitcast(I32),
             )
@@ -73,6 +73,11 @@ def tile_picked_yhlgnn_gate_p_kernel(
         nc.sync.dma_start(out=unit_sb[:], in_=unit.rearrange("(p t) o -> p (t o)", t=PACK))
         for t in range(2, PACK):
             load_own(t)
+
+        warm_in = held.tile([P, 1], F32, name="warm_in")
+        warm_out = held.tile([P, 1], F32, name="warm_out")
+        nc.vector.memset(warm_in[:], 0.0)
+        nc.scalar.activation(warm_out[:], warm_in[:], ACT.Sigmoid)
 
         h_bf = [held.tile([P, PACK * H], BF16, name=f"h_bf{o}", align_bytes=64) for o in range(PASSES)]
         h_codes = [held.tile([P, H], U32, name=f"h_codes{o}", align_bytes=64) for o in range(PASSES)]

@@ -51,28 +51,33 @@ def tile_picked_yhlgnn_gate_p_kernel(
             src = x_words[o].rearrange("p c r -> p (c r)").bitcast(I32)
             nc.sync.dma_start(out=words[o][:].bitcast(I32), in_=src)
 
+        def load_scales(o):
+            for q in range(4):
+                first = 32 * q + 4 * o
+                nc.sync.dma_start(
+                    out=scales[first : first + 4, :].bitcast(I32),
+                    in_=x_scales[o, 4 * q : 4 * q + 4, :].bitcast(I32),
+                )
+
         def load_own(t):
             nc.sync.dma_start(out=hv_own[t][:, S:], in_=own_rows[:, t, :])
 
         nc.gpsimd.memset(scales[:].bitcast(I32), 0)
         load_h(0)
-        for q in range(4):
-            nc.sync.dma_start(
-                out=scales[32 * q : 32 * q + 4 * PASSES, :].bitcast(I32),
-                in_=x_scales[:, 4 * q : 4 * q + 4, :].bitcast(I32),
-            )
+        load_scales(0)
         nc.sync.dma_start(offs_sb[:], offs)
         load_words(0)
+        load_scales(1)
         load_h(1)
         load_words(1)
         nc.sync.dma_start(out=w_raw[:], in_=w1.rearrange("(p j) n -> p j n", j=PACK))
         nc.sync.dma_start(ven_sb[:], ven)
         load_own(0)
-        nc.sync.dma_start(coc_sb[:], coc)
         load_own(1)
+        nc.sync.dma_start(coc_sb[:], coc)
+        load_own(2)
+        load_own(3)
         nc.sync.dma_start(out=unit_sb[:], in_=unit.rearrange("(p t) o -> p (t o)", t=PACK))
-        for t in range(2, PACK):
-            load_own(t)
 
         warm_in = held.tile([P, 1], F32, name="warm_in")
         warm_out = held.tile([P, 1], F32, name="warm_out")
@@ -88,11 +93,15 @@ def tile_picked_yhlgnn_gate_p_kernel(
         def deal_h(o):
             dst = h_bf[o][:].rearrange("p (t m j) -> p m j t", t=PACK, j=PACK)
             src = h_raw[o][:].rearrange("p j (m t) -> p m j t", t=PACK)
-            nc.vector.tensor_copy(dst[:, :, :, : PACK - 1], src[:, :, :, : PACK - 1])
-            nc.scalar.copy(dst[:, :, :, PACK - 1], src[:, :, :, PACK - 1])
+            nc.vector.tensor_copy(dst[:, :, :, :2], src[:, :, :, :2])
+            nc.scalar.copy(dst[:, :, :, 2:], src[:, :, :, 2:])
 
         def quantize(codes, scale_bytes, values):
             nc.vector.quantize_mx(out=codes.bitcast(FP8X4), scales=scale_bytes, in_=values)
+
+        def quantize_h(o, u):
+            cols = slice(u * 2 * P, (u + 1) * 2 * P)
+            quantize(h_codes[o][:, cols], h_scales[o][:, cols], h_bf[o][:, PACK * cols.start : PACK * cols.stop])
 
         halves = [slice(0, S // 2), slice(S // 2, S)]
         spans = [(0, halves[0]), (1, halves[0]), (0, halves[1]), (1, halves[1]), (2, slice(0, S)), (3, slice(0, S))]
@@ -112,12 +121,14 @@ def tile_picked_yhlgnn_gate_p_kernel(
                 )
 
         deal_h(0)
-        quantize(h_codes[0][:], h_scales[0][:], h_bf[0][:])
+        quantize_h(0, 0)
+        quantize_h(0, 1)
         nc.vector.tensor_copy(x_codes[0][:], words[0][:].indirect(offs_sb[:]))
         nc.vector.tensor_copy(x_bytes[:], scales[:].indirect(offs_sb[:]))
         scores(0)
         deal_h(1)
-        quantize(h_codes[1][:], h_scales[1][:], h_bf[1][:])
+        quantize_h(1, 0)
+        quantize_h(1, 1)
         for c in halves:
             nc.vector.tensor_copy(x_codes[1][:, c], words[1][:].indirect(offs_sb[:, c.start // 16 : c.stop // 16]))
         scores(1)
@@ -133,10 +144,12 @@ def tile_picked_yhlgnn_gate_p_kernel(
 
         def bound(k):
             t, c = spans[k]
-            nc.scalar.activation(venue_aff[t][:, V + c.start : V + c.stop], y[k][:], ACT.Tanh)
+            members = venue_aff[t][:, V:].rearrange("p (d v) -> p d v", d=2)
+            scores_by_member = y[k][:].rearrange("p (v d) -> p d v", d=2)
+            nc.scalar.activation(members[:, :, c.start // 2 : c.stop // 2], scores_by_member, ACT.Tanh)
 
         def larger(t):
-            pairs = venue_aff[t][:, V:].rearrange("p (v d) -> p d v", d=2)
+            pairs = venue_aff[t][:, V:].rearrange("p (d v) -> p d v", d=2)
             nc.vector.tensor_tensor(venue_aff[t][:, :V], pairs[:, 0, :], pairs[:, 1, :], ALU.max)
 
         def fetch_add(t):
@@ -177,10 +190,11 @@ def tile_picked_yhlgnn_gate_p_kernel(
         hid_codes = [held.tile([P, w], U32, name=f"hid_codes{a}", align_bytes=64) for a, w in enumerate(widths)]
         hid_scales = [held.tile([P, w], U8, name=f"hid_scales{a}", align_bytes=64) for a, w in enumerate(widths)]
 
-        def weave(a, copy):
-            interleave(copy, hid_bf[a][:], hid_rows[:, :, piece[a]])
+        def weave(a, copy, lo, hi):
+            first = piece[a].start
+            interleave(copy, hid_bf[a][:, PACK * lo : PACK * hi], hid_rows[:, :, first + lo : first + hi])
 
-        def finish(a):
+        def finish(a, copy):
             quantize(hid_codes[a][:], hid_scales[a][:], hid_bf[a][:])
             acc = psum.tile([P, widths[a]], F32, name=f"acc{a}", tag=f"y{a}")
             nc.tensor.matmul_mx(
@@ -193,7 +207,7 @@ def tile_picked_yhlgnn_gate_p_kernel(
                 stop=True,
             )
             result = held.tile([P, widths[a]], F32, name=f"result{a}")
-            nc.scalar.copy(result[:], acc[:])
+            copy(result[:], acc[:])
             nc.sync.dma_start(out=out[:, piece[a]], in_=result[:])
 
         interleave(nc.vector.tensor_copy, w_bf[:], w_raw[:])
@@ -202,27 +216,22 @@ def tile_picked_yhlgnn_gate_p_kernel(
         larger(0)
         larger(1)
         fetch_add(0)
+        fetch(1)
         larger(2)
-        fetch_add(1)
-        gates(0, whole)
-        fetch(2)
         larger(3)
-        fetch_add(3)
+        add(1)
+        gates(0, whole)
+        fetch_add(2)
         gates(1, whole)
-        add(2)
-        hidden(0, whole)
-        gates(3, piece[0])
-        gates(2, piece[0])
-        hidden(1, whole)
+        fetch_add(3)
+        gates(2, whole)
+        gates(3, halves[0])
         gates(3, halves[1])
-        hidden(3, piece[0])
-        hidden(2, piece[0])
-        gates(2, halves[1])
-        weave(0, nc.vector.tensor_copy)
-        hidden(3, halves[1])
-        hidden(2, halves[1])
-        weave(1, nc.scalar.copy)
-        finish(0)
-        weave(2, nc.vector.tensor_copy)
-        finish(1)
-        finish(2)
+        for t in range(PACK): hidden(t, halves[0])
+        weave(0, nc.scalar.copy, 0, 256)
+        for t in range(PACK): hidden(t, halves[1])
+        weave(1, nc.scalar.copy, 0, 128)
+        finish(0, nc.scalar.copy)
+        weave(2, nc.vector.tensor_copy, 0, 128)
+        finish(1, nc.scalar.copy)
+        finish(2, nc.vector.tensor_copy)

from contextlib import ExitStack

import concourse.mybir as mybir

K, T, S, N, H, V = 1024, 2048, 512, 128, 512, 256

F32 = mybir.dt.float32
BF16 = mybir.dt.bfloat16
I32 = mybir.dt.int32
U32 = mybir.dt.uint32
U16 = mybir.dt.uint16
U8 = mybir.dt.uint8
FP8X4 = mybir.dt.float8_e4m3fn_x4
ALU = mybir.AluOpType
ACT = mybir.ActivationFunctionType

P = 128
PACK = 4
PASSES = K // (P * PACK)
PIECES = 2
PIECE = S // PIECES

FLOPS = 2 * K * H * S + 2 * H * N * S


def tile_picked_yhlgnn_gate_p_kernel(
    tc, x_words, x_scales, hT, own, unit, w1, offs, ven, coc, out
):
    nc = tc.nc
    with ExitStack() as ctx:
        held = ctx.enter_context(tc.tile_pool(name="held", bufs=1))
        psum = ctx.enter_context(tc.psum_pool(name="psum", bufs=1))

        offs_sb = held.tile([P, S // 16], U16, name="offs_sb")
        ven_sb = held.tile([P, S // 16], U16, name="ven_sb")
        coc_sb = held.tile([P, S // 16], U16, name="coc_sb")
        h_raw = [held.tile([P, PACK, H], F32, name=f"h_raw{o}") for o in range(PASSES)]
        words = [held.tile([P, T], U32, name=f"words{o}") for o in range(PASSES)]
        scales = held.tile([P, T], U8, name="scales")
        hv_own = [held.tile([P, 2 * S], F32, name=f"hv_own{t}") for t in range(PACK)]
        w_raw = held.tile([P, PACK, N], F32, name="w_raw")
        unit_sb = held.tile([P, PACK], F32, name="unit_sb")

        own_rows = own.rearrange("(p t) j -> p t j", t=PACK)

        def load_h(o):
            rows = hT[o * P * PACK : (o + 1) * P * PACK, :]
            nc.sync.dma_start(out=h_raw[o][:], in_=rows.rearrange("(p j) c -> p j c", j=PACK))

        def load_words(o):
            src = x_words[o].rearrange("p c r -> p (c r)").bitcast(I32)
            nc.sync.dma_start(out=words[o][:].bitcast(I32), in_=src)

        def load_scales(o):
            for q in range(4):
                first = 32 * q + 4 * o
                nc.sync.dma_start(
                    out=scales[first : first + 4, :].bitcast(I32),
                    in_=x_scales[o, 4 * q : 4 * q + 4, :].bitcast(I32),
                )

        def load_own(t):
            nc.sync.dma_start(out=hv_own[t][:, S:], in_=own_rows[:, t, :])

        nc.gpsimd.memset(scales[:].bitcast(I32), 0)
        load_h(0)
        load_scales(0)
        nc.sync.dma_start(offs_sb[:], offs)
        load_words(0)
        load_scales(1)
        load_h(1)
        load_words(1)
        nc.sync.dma_start(out=w_raw[:], in_=w1.rearrange("(p j) n -> p j n", j=PACK))
        nc.sync.dma_start(ven_sb[:], ven)
        load_own(0)
        load_own(1)
        nc.sync.dma_start(coc_sb[:], coc)
        load_own(2)
        load_own(3)
        nc.sync.dma_start(out=unit_sb[:], in_=unit.rearrange("(p t) o -> p (t o)", t=PACK))

        warm_in = held.tile([P, 1], F32, name="warm_in")
        warm_out = held.tile([P, 1], F32, name="warm_out")
        nc.vector.memset(warm_in[:], 0.0)
        nc.scalar.activation(warm_out[:], warm_in[:], ACT.Sigmoid)

        h_bf = [held.tile([P, PACK * H], BF16, name=f"h_bf{o}", align_bytes=64) for o in range(PASSES)]
        h_codes = [held.tile([P, H], U32, name=f"h_codes{o}", align_bytes=64) for o in range(PASSES)]
        h_scales = [held.tile([P, H], U8, name=f"h_scales{o}", align_bytes=64) for o in range(PASSES)]
        x_codes = [held.tile([P, S], U32, name=f"x_codes{o}", align_bytes=64) for o in range(PASSES)]
        x_bytes = held.tile([P, S], U8, name="x_bytes", align_bytes=64)

        def deal_h(o):
            dst = h_bf[o][:].rearrange("p (t m j) -> p m j t", t=PACK, j=PACK)
            src = h_raw[o][:].rearrange("p j (m t) -> p m j t", t=PACK)
            nc.vector.tensor_copy(dst[:, :, :, :2], src[:, :, :, :2])
            nc.scalar.copy(dst[:, :, :, 2:], src[:, :, :, 2:])

        def quantize(codes, scale_bytes, values):
            nc.vector.quantize_mx(out=codes.bitcast(FP8X4), scales=scale_bytes, in_=values)

        def quantize_h(o, u):
            cols = slice(u * 2 * P, (u + 1) * 2 * P)
            quantize(h_codes[o][:, cols], h_scales[o][:, cols], h_bf[o][:, PACK * cols.start : PACK * cols.stop])

        halves = [slice(0, S // 2), slice(S // 2, S)]
        spans = [(0, halves[0]), (1, halves[0]), (0, halves[1]), (1, halves[1]), (2, slice(0, S)), (3, slice(0, S))]
        y = [psum.tile([P, c.stop - c.start], F32, name=f"y{k}") for k, (t, c) in enumerate(spans)]

        def scores(o):
            for k, (t, c) in enumerate(spans):
                cols = slice(t * P, (t + 1) * P)
                nc.tensor.matmul_mx(
                    out=y[k][:],
                    lhsT=h_codes[o][:, cols].bitcast(FP8X4),
                    lhsT_scale=h_scales[o][:, cols],
                    rhs=x_codes[o][:, c].bitcast(FP8X4),
                    rhs_scale=x_bytes[4 * o :, c],
                    start=(o == 0),
                    stop=(o == PASSES - 1),
                )

        deal_h(0)
        quantize_h(0, 0)
        quantize_h(0, 1)
        nc.vector.tensor_copy(x_codes[0][:], words[0][:].indirect(offs_sb[:]))
        nc.vector.tensor_copy(x_bytes[:], scales[:].indirect(offs_sb[:]))
        scores(0)
        deal_h(1)
        quantize_h(1, 0)
        quantize_h(1, 1)
        for c in halves:
            nc.vector.tensor_copy(x_codes[1][:, c], words[1][:].indirect(offs_sb[:, c.start // 16 : c.stop // 16]))
        scores(1)

        venue_aff = [held.tile([P, V + S], F32, name=f"venue_aff{t}") for t in range(PACK)]
        gate = [held.tile([P, S], F32, name=f"gate{t}") for t in range(PACK)]
        picked = held.tile([P, S], F32, name="picked")
        hid_rows = held.tile([P, PACK, S], BF16, name="hid_rows")
        widths = [256,128,128]
        starts = [sum(widths[:a]) for a in range(len(widths))]
        whole = slice(0, S)
        piece = [slice(c, c + w) for c, w in zip(starts, widths)]

        def bound(k):
            t, c = spans[k]
            members = venue_aff[t][:, V:].rearrange("p (d v) -> p d v", d=2)
            scores_by_member = y[k][:].rearrange("p (v d) -> p d v", d=2)
            nc.scalar.activation(members[:, :, c.start // 2 : c.stop // 2], scores_by_member, ACT.Tanh)

        def larger(t):
            pairs = venue_aff[t][:, V:].rearrange("p (d v) -> p d v", d=2)
            nc.vector.tensor_tensor(venue_aff[t][:, :V], pairs[:, 0, :], pairs[:, 1, :], ALU.max)

        def fetch_add(t):
            nc.vector.tensor_tensor(
                hv_own[t][:, :S], venue_aff[t][:].indirect(ven_sb[:]), hv_own[t][:, S:], ALU.add
            )

        def fetch(t):
            nc.scalar.activation(picked[:], venue_aff[t][:].indirect(ven_sb[:]), ACT.Copy)

        def add(t):
            nc.vector.tensor_tensor(hv_own[t][:, :S], picked[:], hv_own[t][:, S:], ALU.add)

        def gates(t, cols):
            entries = coc_sb[:, cols.start // 16 : cols.stop // 16]
            nc.scalar.activation(gate[t][:, cols], hv_own[t][:].indirect(entries), ACT.Sigmoid)

        def hidden(t, cols):
            nc.vector.scalar_tensor_tensor(
                out=hid_rows[:, t, cols],
                in0=hv_own[t][:, cols],
                scalar=unit_sb[:, t : t + 1],
                in1=gate[t][:, cols],
                op0=ALU.mult,
                op1=ALU.mult,
            )

        def interleave(copy, dst, src):
            copy(
                dst.rearrange("p (c i t) -> p c t i", i=4, t=PACK),
                src.rearrange("p t (c i) -> p c t i", i=4),
            )

        w_bf = held.tile([P, PACK * N], BF16, name="w_bf", align_bytes=64)
        w_codes = held.tile([P, N], U32, name="w_codes", align_bytes=64)
        w_scales = held.tile([P, N], U8, name="w_scales", align_bytes=64)
        hid_bf = [held.tile([P, PACK * w], BF16, name=f"hid_bf{a}", align_bytes=64) for a, w in enumerate(widths)]
        hid_codes = [held.tile([P, w], U32, name=f"hid_codes{a}", align_bytes=64) for a, w in enumerate(widths)]
        hid_scales = [held.tile([P, w], U8, name=f"hid_scales{a}", align_bytes=64) for a, w in enumerate(widths)]

        def weave(a, copy, lo, hi):
            first = piece[a].start
            interleave(copy, hid_bf[a][:, PACK * lo : PACK * hi], hid_rows[:, :, first + lo : first + hi])

        def finish(a, copy):
            quantize(hid_codes[a][:], hid_scales[a][:], hid_bf[a][:])
            acc = psum.tile([P, widths[a]], F32, name=f"acc{a}", tag=f"y{a}")
            nc.tensor.matmul_mx(
                out=acc[:],
                lhsT=w_codes[:].bitcast(FP8X4),
                lhsT_scale=w_scales[:],
                rhs=hid_codes[a][:].bitcast(FP8X4),
                rhs_scale=hid_scales[a][:],
                start=True,
                stop=True,
            )
            result = held.tile([P, widths[a]], F32, name=f"result{a}")
            copy(result[:], acc[:])
            nc.sync.dma_start(out=out[:, piece[a]], in_=result[:])

        interleave(nc.vector.tensor_copy, w_bf[:], w_raw[:])
        for k in range(len(spans)): bound(k)
        quantize(w_codes[:], w_scales[:], w_bf[:])
        larger(0)
        larger(1)
        fetch_add(0)
        fetch(1)
        larger(2)
        larger(3)
        add(1)
        gates(0, whole)
        fetch_add(2)
        gates(1, whole)
        fetch_add(3)
        gates(2, whole)
        gates(3, halves[0])
        gates(3, halves[1])
        for t in range(PACK): hidden(t, halves[0])
        weave(0, nc.scalar.copy, 0, 256)
        for t in range(PACK): hidden(t, halves[1])
        weave(1, nc.scalar.copy, 0, 128)
        finish(0, nc.scalar.copy)
        weave(2, nc.vector.tensor_copy, 0, 128)
        finish(1, nc.scalar.copy)
        finish(2, nc.vector.tensor_copy)
